import numpy as np
import ml_dtypes


def mxq(x, axis, fmt="e4m3"):
    dtype, down = {"e4m3": (ml_dtypes.float8_e4m3fn, 7), "e5m2": (ml_dtypes.float8_e5m2, 14)}[fmt]
    v = np.moveaxis(np.asarray(x, np.float32).astype(ml_dtypes.bfloat16).astype(np.float64), axis, -1)
    blocks = v.reshape(v.shape[:-1] + (-1, 32))
    amax = np.abs(blocks).max(-1, keepdims=True)
    byte = np.maximum(np.where(amax > 0, np.frexp(amax)[1] - 1 + 127, 0) - down, 1)
    scale = np.exp2(byte - 127.0)
    codes = (blocks / scale).astype(np.float32).astype(dtype).astype(np.float64)
    return np.moveaxis((codes * scale).reshape(v.shape), -1, axis)


WIDE = False


def mx_kscale(k):
    if not WIDE:
        return np.ones(k)
    levels = np.array([10, -10, 5, -5, 0])
    if k % 512:
        return np.exp2(np.random.permutation(np.resize(levels, k // 32))).repeat(32)
    a = np.empty((k // 512, 16))
    for p in range(k // 512):
        a[p, :8] = np.random.permutation(np.resize(levels, 8))
        for g in range(8):
            far = levels[np.abs(levels - a[p, g]) >= 10]
            a[p, g + 8] = far[np.random.randint(len(far))]
    return np.exp2(a.ravel()).repeat(32)


def f64(x):
    return np.asarray(x).astype(np.float64)


def striped(idx):
    return np.tile(idx.reshape(-1, 16).T, (8, 1)).astype(np.uint16)


def unstriped(offs):
    return offs[:16].T.reshape(-1).astype(np.int64)


E2M1 = np.array([0.0, 0.5, 1.0, 1.5, 2.0, 3.0, 4.0, 6.0, -0.0, -0.5, -1.0, -1.5, -2.0, -3.0, -4.0, -6.0])


def pack_weight(w, fmt):
    k, n = w.shape
    w = f64(np.asarray(w, np.float32).astype(ml_dtypes.bfloat16)).reshape(k // 32, 32, n)
    amax = np.abs(w).max(1)
    if fmt == "e4m3":
        byte = np.frexp(amax)[1] - 1 + 127 - 7
    else:
        mant, ex = np.frexp(amax / 6.0)
        byte = np.where(mant > 0.5, ex, ex - 1) + 127
    byte = np.clip(np.where(amax > 0, byte, 1), 1, 254)
    scaled = (w * np.exp2(127.0 - byte)[:, None, :]).reshape(k, n).astype(np.float32)
    by_word = np.ascontiguousarray(scaled.reshape(k // 512, 128, 4, n).transpose(0, 1, 3, 2))
    if fmt == "e4m3":
        words = by_word.astype(ml_dtypes.float8_e4m3fn).view(np.uint8)
    else:
        c = by_word.astype(ml_dtypes.float4_e2m1fn).view(np.uint8) & 0xF
        words = (c[..., 0::2] | (c[..., 1::2] << 4)).reshape(k // 512, 128, 2 * n)
    return np.ascontiguousarray(words), np.ascontiguousarray(byte.astype(np.uint8).reshape(k // 512, 16, n))


def unpack_weight(words, scales, fmt):
    g, _, n = scales.shape
    words = np.ascontiguousarray(words).reshape(g, 128, n, -1)
    if fmt == "e4m3":
        vals = words.view(ml_dtypes.float8_e4m3fn).astype(np.float64)
    else:
        nib = np.empty((g, 128, n, 4), np.uint8)
        nib[..., 0::2] = words & 0xF
        nib[..., 1::2] = words >> 4
        vals = E2M1[nib]
    vals = vals * np.repeat(np.exp2(scales.astype(np.float64) - 127.0), 8, axis=1)[..., None]
    return vals.transpose(0, 1, 3, 2).reshape(g * 512, n)


def gelu(v):
    return 0.5 * v * (1.0 + np.tanh(np.sqrt(2.0 / np.pi) * (v + 0.044715 * v**3)))


def striped8(idx):
    return np.concatenate([v.reshape(-1, 16).T for v in idx]).astype(np.uint16)


def unstriped8(offs):
    return np.stack([offs[16 * g:16 * g + 16].T.reshape(-1) for g in range(8)]).astype(np.int64)


def heads(h, wgt, idx8):
    r = np.arange(h.shape[0])
    return wgt[r // 4 % 128] * h[r[:, None], idx8[r % 512 // 64]]


def put_heads(h, wgs, idx8, t2):
    r = np.arange(h.shape[0])
    page = np.zeros((h.shape[0], t2))
    page[r[:, None], idx8[r % 512 // 64]] = wgs[r // 4 % 128] * h
    return page


K, H, N, T, S, P, T2 = 512, 1024, 768, 4096, 1024, 1024, 2048


def setup_inputs():
    n = np.random.standard_normal
    s = mx_kscale(K)[:, None]
    u = mx_kscale(H)[:, None]
    d = {}
    d["tab_words"], d["tab_scales"] = pack_weight(n((K, T)) * s, "e4m3")
    d["offs"] = striped(np.random.permutation(T)[:S])
    d["offs2"] = striped8(np.stack([np.random.permutation(T2)[:S] for _ in range(8)]))
    d["offs3"] = striped8(np.stack([np.random.permutation(T2)[:P] for _ in range(8)]))
    d["w1"] = (n((K, H)) / s * u.T / K**0.5).astype(np.float32)
    d["w2_words"], d["w2_scales"] = pack_weight(2.2 * n((K, H)) / s / K**0.5, "e2m1")
    d["wgs"] = np.repeat(np.random.uniform(0.5, 2.0, (8, S)), 16, axis=0).astype(np.float32)
    d["wgt"] = np.repeat(np.random.uniform(0.5, 2.0, (8, P)), 16, axis=0).astype(np.float32)
    d["paste"] = (0.9 * n((H, P)) * u).astype(np.float32)
    d["w3_words"], d["w3_scales"] = pack_weight(0.9 * n((H, N)) / u / H**0.5, "e2m1")
    d["w4"] = (0.6 * n((H, N)) / u / H**0.5).astype(np.float32)
    return d


def reference(tab_words, tab_scales, offs, offs2, offs3, w1, w2_words, w2_scales,
              wgs, wgt, paste, w3_words, w3_scales, w4):
    v = unpack_weight(tab_words, tab_scales, "e4m3")[:, unstriped(offs)]
    a = mxq(f64(w1), 0, "e4m3").T @ v
    b = unpack_weight(w2_words, w2_scales, "e2m1").T @ v
    h = a / (0.5 + 1.0 / (1.0 + np.exp(-b)))
    page = put_heads(h, f64(wgs), unstriped8(offs2), T2)
    x = heads(page, f64(wgt), unstriped8(offs3))
    z = x + f64(paste)
    zq = mxq(z, 0, "e4m3")
    mq = mxq(np.abs(z), 0, "e4m3")
    y = unpack_weight(w3_words, w3_scales, "e2m1").T @ zq
    e = mxq(f64(w4), 0, "e4m3").T @ mq
    return np.tanh(y) + e

@@ -1,0 +1,258 @@
+import math
+from contextlib import ExitStack
+
+import concourse.mybir as mybir
+
+K, H, N, T, S, M, T2 = 512, 1024, 768, 4096, 1024, 1024, 2048
+FLOPS = 2 * (2 * K * H * S + 2 * H * N * M)
+
+F32 = mybir.dt.float32
+BF16 = mybir.dt.bfloat16
+I32 = mybir.dt.int32
+U32 = mybir.dt.uint32
+U16 = mybir.dt.uint16
+U8 = mybir.dt.uint8
+FP8X4 = mybir.dt.float8_e4m3fn_x4
+FP4X4 = mybir.dt.float4_e2m1fn_x4
+ALU = mybir.AluOpType
+ACT = mybir.ActivationFunctionType
+
+P = 128
+PACK = 4
+PASS = P * PACK
+PASSES = H // PASS
+ROW_TILES = H // P
+BANK = 512
+CHUNK = 256
+LIST = 16
+
+
+def tile_list_rework_pad_scores_kernel(
+    tc, tab_words, tab_scales, offs, offs2, offs3, w1, w2_words, w2_scales, wgs, wgt, paste, w3_words, w3_scales, w4, out
+):
+    nc = tc.nc
+    with ExitStack() as ctx:
+        lists = ctx.enter_context(tc.tile_pool(name="lists", bufs=1))
+        keep = ctx.enter_context(tc.tile_pool(name="keep", bufs=1))
+        ring = ctx.enter_context(tc.tile_pool(name="ring", bufs=2))
+        psum = ctx.enter_context(tc.psum_pool(name="psum", bufs=8))
+
+        idx = lists.tile([P, S // LIST], U16, name="idx")
+        idx2 = lists.tile([P, S // LIST], U16, name="idx2")
+        idx3 = lists.tile([P, M // LIST], U16, name="idx3")
+
+        def load_scale_rows(queue, plane, rows):
+            for q in range(4):
+                queue.dma_start(
+                    out=plane[32 * q : 32 * q + 4].bitcast(I32),
+                    in_=rows[:, 4 * q : 4 * q + 4, :].rearrange("a r c -> r a c").bitcast(I32),
+                )
+
+        tab_plane = keep.tile([P, T], U8, name="tab_plane", align_bytes=64)
+        w2_plane_raw = keep.tile([P, 1, H], U8, name="w2_plane_raw", align_bytes=64)
+        w3_plane = keep.tile([P, PASSES, N], U8, name="w3_plane", align_bytes=64)
+        nc.vector.memset(tab_plane[:].bitcast(I32), 0)
+        nc.vector.memset(w2_plane_raw[:].bitcast(I32), 0)
+        nc.vector.memset(w3_plane[:].bitcast(I32), 0)
+        pages = [keep.tile([P, T2], F32, name="page%d" % n) for n in range(2)]
+        for page in pages:
+            nc.vector.memset(page[:], 0.0)
+        shift = keep.tile([P, 1], F32, name="shift")
+        nc.vector.memset(shift[:], 1.0)
+        nc.vector.tensor_scalar(shift[:], shift[:], 0.5 * math.log(3.0), None, ALU.mult)
+
+        nc.sync.dma_start(idx[:], offs)
+        w2_raw = keep.tile([P, 2 * H], U8, name="w2_raw")
+        nc.sync.dma_start(out=w2_raw[:].bitcast(I32), in_=w2_words[0].bitcast(I32))
+        load_scale_rows(nc.sync, tab_plane[:].rearrange("p (a t) -> p a t", a=1), tab_scales)
+        tab = ring.tile([P, T], I32, name="tab", tag="wide")
+        nc.sync.dma_start(out=tab[:], in_=tab_words[0].rearrange("p t i -> p (t i)").bitcast(I32))
+        w1_rows = w1.rearrange("(p j) r -> p j r", j=PACK)
+        w1_raw = []
+        factor_s = keep.tile([P, S], F32, name="factor_s")
+        factor_t = keep.tile([P, M], F32, name="factor_t")
+        for b in range(PASSES):
+            raw = ring.tile([P, PACK, PASS], F32, name="w1_raw", tag="raw")
+            nc.sync.dma_start(out=raw[:], in_=w1_rows[:, :, b * PASS : (b + 1) * PASS])
+            w1_raw.append(raw)
+            if b == 0:
+                load_scale_rows(nc.sync, w2_plane_raw[:], w2_scales)
+                nc.sync.dma_start(idx2[:], offs2)
+                nc.sync.dma_start(out=factor_s[:], in_=wgs)
+        nc.sync.dma_start(idx3[:], offs3)
+        nc.sync.dma_start(out=factor_t[:], in_=wgt)
+
+        w2_codes = keep.tile([P, 2 * H], U8, name="w2_codes", align_bytes=64)
+        w2_plane = keep.tile([P, H], U8, name="w2_plane", align_bytes=64)
+        nc.vector.tensor_copy(
+            out=w2_codes[:].rearrange("p (b t q e) -> p b t q e", b=PASSES, t=PACK, e=2),
+            in_=w2_raw[:].rearrange("p (b q t e) -> p b t q e", b=PASSES, t=PACK, e=2),
+        )
+        nc.vector.tensor_copy(
+            out=w2_plane[:].rearrange("p (b t q) -> p b t q", b=PASSES, t=PACK),
+            in_=w2_plane_raw[:, 0, :].rearrange("p (b q t) -> p b t q", b=PASSES, t=PACK),
+        )
+
+        v_codes = keep.tile([P, S], U32, name="v_codes", align_bytes=64)
+        v_plane = keep.tile([P, S], U8, name="v_plane", align_bytes=64)
+        nc.vector.tensor_copy(out=v_plane[:], in_=tab_plane[:].indirect(idx[:]))
+        for s0 in range(0, S, BANK):
+            entries = idx[:, s0 // LIST : (s0 + BANK) // LIST]
+            nc.vector.tensor_copy(out=v_codes[:, s0 : s0 + BANK], in_=tab[:].bitcast(U32).indirect(entries))
+
+        w1_codes = keep.tile([P, H], U32, name="w1_codes", align_bytes=64)
+        w1_plane = keep.tile([P, H], U8, name="w1_plane", align_bytes=64)
+
+        def quantise_w1(b, t0, t1):
+            width = (t1 - t0) * P
+            rounded = ring.tile([P, width * PACK], BF16, name="w1_rounded", tag="rounded", align_bytes=64)
+            nc.scalar.copy(
+                out=rounded[:].rearrange("p (t q j) -> p q j t", q=P, j=PACK),
+                in_=w1_raw[b][:].rearrange("p j (q t) -> p q j t", t=PACK)[:, :, :, t0:t1],
+            )
+            cols = slice(b * PASS + t0 * P, b * PASS + t1 * P)
+            nc.vector.quantize_mx(out=w1_codes[:, cols].bitcast(FP8X4), scales=w1_plane[:, cols], in_=rounded[:])
+
+        quantise_w1(0, 0, 1)
+        nc.scalar.mul(factor_s[:], factor_s[:], -2.0 / 3.0)
+
+        def features(k):
+            cols = slice(k * P, (k + 1) * P)
+            curve = ring.tile([P, S], F32, name="curve")
+            feat = ring.tile([P, S], F32, name="feat")
+            for s0 in range(0, S, BANK):
+                span = slice(s0, s0 + BANK)
+                gate = psum.tile([P, BANK], F32, name="gate", tag="bank")
+                nc.tensor.matmul_mx(
+                    out=gate[:], lhsT=w2_codes[:, 2 * k * P : 2 * (k + 1) * P].bitcast(FP4X4), lhsT_scale=w2_plane[:, cols],
+                    rhs=v_codes[:, span].bitcast(FP8X4), rhs_scale=v_plane[:, span], start=True, stop=True,
+                )
+                lin = psum.tile([P, BANK], F32, name="lin", tag="bank")
+                nc.tensor.matmul_mx(
+                    out=lin[:], lhsT=w1_codes[:, cols].bitcast(FP8X4), lhsT_scale=w1_plane[:, cols],
+                    rhs=v_codes[:, span].bitcast(FP8X4), rhs_scale=v_plane[:, span], start=True, stop=True,
+                )
+                nc.scalar.activation(curve[:, span], gate[:], ACT.Tanh, bias=shift[:], scale=0.5)
+                nc.vector.scalar_tensor_tensor(feat[:, span], curve[:, span], -2.0, lin[:], ALU.add, ALU.mult)
+            return feat
+
+        def put(k, feat):
+            width = BANK if k == 0 else S
+            for s0 in range(0, S, width):
+                entries = idx2[:, s0 // LIST : (s0 + width) // LIST]
+                nc.vector.tensor_tensor(
+                    pages[k % 2][:].indirect(entries), feat[:, s0 : s0 + width], factor_s[:, s0 : s0 + width], ALU.mult
+                )
+
+        def pick(k, picked, m0, width):
+            entries = idx3[:, m0 // LIST : (m0 + width) // LIST]
+            nc.vector.tensor_tensor(
+                picked[:, k % PACK, m0 : m0 + width], pages[k % 2][:].indirect(entries), factor_t[:, m0 : m0 + width], ALU.mult
+            )
+
+        z_codes = [keep.tile([P, M], U32, name="z_codes%d" % b, align_bytes=64) for b in range(PASSES)]
+        z_plane = [keep.tile([P, M], U8, name="z_plane%d" % b, align_bytes=64) for b in range(PASSES)]
+        mag_codes = [keep.tile([P, M], U32, name="mag_codes%d" % b, align_bytes=64) for b in range(PASSES)]
+        mag_plane = [keep.tile([P, M], U8, name="mag_plane%d" % b, align_bytes=64) for b in range(PASSES)]
+
+        def add_paste(picked, offset, m0):
+            z = ring.tile([P, CHUNK * PACK], BF16, name="z", bufs=4, align_bytes=64)
+            mag = ring.tile([P, CHUNK * PACK], BF16, name="mag", bufs=4, align_bytes=64)
+            nc.vector.tensor_tensor(
+                z[:].rearrange("p (c i t) -> p c t i", i=4, t=PACK),
+                picked[:, :, m0 : m0 + CHUNK].rearrange("p t (c i) -> p c t i", i=4),
+                offset[:, :, m0 : m0 + CHUNK].rearrange("p t (c i) -> p c t i", i=4),
+                ALU.add,
+            )
+            nc.scalar.activation(mag[:], z[:], ACT.Abs)
+            return z, mag
+
+        def quantise(values, codes, plane, m0):
+            nc.vector.quantize_mx(out=codes[:, m0 : m0 + CHUNK].bitcast(FP8X4), scales=plane[:, m0 : m0 + CHUNK], in_=values[:])
+
+        def load_paste(b):
+            offset = ring.tile([P, PACK, M], F32, name="offset", tag="wide")
+            nc.sync.dma_start(out=offset[:], in_=paste[b * PASS : (b + 1) * PASS, :].rearrange("(p t) m -> p t m", t=PACK))
+            return offset
+
+        w4_codes = keep.tile([P, PASSES * N], U32, name="w4_codes", align_bytes=64)
+        w4_plane = keep.tile([P, PASSES * N], U8, name="w4_plane", align_bytes=64)
+
+        def load_w4(b):
+            raw = ring.tile([P, PACK, N], F32, name="w4_raw", tag="raw")
+            nc.sync.dma_start(out=raw[:], in_=w4[b * PASS : (b + 1) * PASS, :].rearrange("(p j) n -> p j n", j=PACK))
+            return raw
+
+        def quantise_w4(b, raw):
+            half = N // 2
+            for n0 in range(0, N, half):
+                rounded = ring.tile([P, half * PACK], BF16, name="w4_rounded", tag="rounded", align_bytes=64)
+                nc.scalar.copy(
+                    out=rounded[:].rearrange("p (c i j) -> p c j i", i=4, j=PACK),
+                    in_=raw[:, :, n0 : n0 + half].rearrange("p j (c i) -> p c j i", i=4),
+                )
+                cols = slice(b * N + n0, b * N + n0 + half)
+                nc.vector.quantize_mx(out=w4_codes[:, cols].bitcast(FP8X4), scales=w4_plane[:, cols], in_=rounded[:])
+
+        w3_codes = keep.tile([P, PASSES, 2 * N], U8, name="w3_codes", align_bytes=64)
+
+        def finish_pass(b, picked, offset, last_tile):
+            waiting = None
+            for m0 in range(0, M, CHUNK):
+                if last_tile is not None:
+                    pick(last_tile, picked, m0, CHUNK)
+                z, mag = add_paste(picked, offset, m0)
+                if waiting is not None:
+                    quantise(waiting[0], mag_codes[b], mag_plane[b], waiting[1])
+                quantise(z, z_codes[b], z_plane[b], m0)
+                waiting = (mag, m0)
+            quantise(waiting[0], mag_codes[b], mag_plane[b], waiting[1])
+
+        feats = {0: features(0)}
+        quantise_w1(0, 1, PACK)
+        offsets = [load_paste(0)]
+        picked = {}
+        w4_raw = {}
+        for k in range(ROW_TILES):
+            if k + 1 < ROW_TILES:
+                feats[k + 1] = features(k + 1)
+            put(k, feats[k])
+            if k == 0:
+                quantise_w1(1, 0, PACK)
+                offsets.append(load_paste(1))
+                w4_raw[0] = load_w4(0)
+                w4_raw[1] = load_w4(1)
+                nc.sync.dma_start(out=w3_codes[:].bitcast(I32), in_=w3_words.rearrange("a p c -> p a c").bitcast(I32))
+                load_scale_rows(nc.sync, w3_plane[:], w3_scales)
+            if k >= 1:
+                j = k - 1
+                if j % PACK == 0:
+                    picked[j // PACK] = keep.tile([P, PACK, M], F32, name="picked")
+                pick(j, picked[j // PACK], 0, M)
+                if j == PACK - 1:
+                    finish_pass(0, picked[0], offsets[0], None)
+            if k in (2, 3):
+                quantise_w4(k - 2, w4_raw[k - 2])
+        finish_pass(1, picked[1], offsets[1], ROW_TILES - 1)
+
+        for m0 in range(0, M, BANK):
+            span = slice(m0, m0 + BANK)
+            for n0 in range(0, N, P):
+                signed = psum.tile([P, BANK], F32, name="signed", tag="bank")
+                sized = psum.tile([P, BANK], F32, name="sized", tag="bank")
+                for b in range(PASSES):
+                    nc.tensor.matmul_mx(
+                        out=signed[:], lhsT=w3_codes[:, b, 2 * n0 : 2 * (n0 + P)].bitcast(FP4X4), lhsT_scale=w3_plane[:, b, n0 : n0 + P],
+                        rhs=z_codes[b][:, span].bitcast(FP8X4), rhs_scale=z_plane[b][:, span], start=(b == 0), stop=(b == PASSES - 1),
+                    )
+                for b in range(PASSES):
+                    cols = slice(b * N + n0, b * N + n0 + P)
+                    nc.tensor.matmul_mx(
+                        out=sized[:], lhsT=w4_codes[:, cols].bitcast(FP8X4), lhsT_scale=w4_plane[:, cols],
+                        rhs=mag_codes[b][:, span].bitcast(FP8X4), rhs_scale=mag_plane[b][:, span], start=(b == 0), stop=(b == PASSES - 1),
+                    )
+                bounded = ring.tile([P, BANK], F32, name="bounded", bufs=3)
+                nc.scalar.activation(bounded[:], signed[:], ACT.Tanh)
+                score = ring.tile([P, BANK], F32, name="score", bufs=4)
+                nc.vector.tensor_tensor(score[:], bounded[:], sized[:], ALU.add)
+                nc.sync.dma_start(out=out[n0 : n0 + P, span], in_=score[:])

@@ -51,12 +51,12 @@ def tile_list_rework_pad_scores_kernel(
         tab_plane = keep.tile([P, T], U8, name="tab_plane", align_bytes=64)
         w2_plane_raw = keep.tile([P, 1, H], U8, name="w2_plane_raw", align_bytes=64)
         w3_plane = keep.tile([P, PASSES, N], U8, name="w3_plane", align_bytes=64)
-        nc.vector.memset(tab_plane[:].bitcast(I32), 0)
-        nc.vector.memset(w2_plane_raw[:].bitcast(I32), 0)
-        nc.vector.memset(w3_plane[:].bitcast(I32), 0)
+        nc.gpsimd.memset(tab_plane[:].bitcast(I32), 0)
+        nc.gpsimd.memset(w2_plane_raw[:].bitcast(I32), 0)
         pages = [keep.tile([P, T2], F32, name="page%d" % n) for n in range(2)]
         for page in pages:
-            nc.vector.memset(page[:], 0.0)
+            nc.gpsimd.memset(page[:], 0.0)
+        nc.gpsimd.memset(w3_plane[:].bitcast(I32), 0)
         shift = keep.tile([P, 1], F32, name="shift")
         nc.vector.memset(shift[:], 1.0)
         nc.vector.tensor_scalar(shift[:], shift[:], 0.5 * math.log(3.0), None, ALU.mult)
@@ -67,6 +67,7 @@ def tile_list_rework_pad_scores_kernel(
         load_scale_rows(nc.sync, tab_plane[:].rearrange("p (a t) -> p a t", a=1), tab_scales)
         tab = ring.tile([P, T], I32, name="tab", tag="wide")
         nc.sync.dma_start(out=tab[:], in_=tab_words[0].rearrange("p t i -> p (t i)").bitcast(I32))
+        load_scale_rows(nc.sync, w2_plane_raw[:], w2_scales)
         w1_rows = w1.rearrange("(p j) r -> p j r", j=PACK)
         w1_raw = []
         factor_s = keep.tile([P, S], F32, name="factor_s")
@@ -76,7 +77,6 @@ def tile_list_rework_pad_scores_kernel(
             nc.sync.dma_start(out=raw[:], in_=w1_rows[:, :, b * PASS : (b + 1) * PASS])
             w1_raw.append(raw)
             if b == 0:
-                load_scale_rows(nc.sync, w2_plane_raw[:], w2_scales)
                 nc.sync.dma_start(idx2[:], offs2)
                 nc.sync.dma_start(out=factor_s[:], in_=wgs)
         nc.sync.dma_start(idx3[:], offs3)
@@ -103,23 +103,28 @@ def tile_list_rework_pad_scores_kernel(
         w1_codes = keep.tile([P, H], U32, name="w1_codes", align_bytes=64)
         w1_plane = keep.tile([P, H], U8, name="w1_plane", align_bytes=64)
 
-        def quantise_w1(b, t0, t1):
-            width = (t1 - t0) * P
-            rounded = ring.tile([P, width * PACK], BF16, name="w1_rounded", tag="rounded", align_bytes=64)
-            nc.scalar.copy(
-                out=rounded[:].rearrange("p (t q j) -> p q j t", q=P, j=PACK),
+        curves = [keep.tile([P, S], F32, name="curve%d" % n, align_bytes=64) for n in range(2)]
+        feats = [keep.tile([P, S], F32, name="feat%d" % n, align_bytes=64) for n in range(2)]
+        picked = [keep.tile([P, PACK, M], F32, name="picked%d" % b) for b in range(PASSES)]
+
+        def quantise_w1(b, t0, t1, rounded, copy):
+            copy(
+                out=rounded.rearrange("p (t q j) -> p q j t", q=P, j=PACK),
                 in_=w1_raw[b][:].rearrange("p j (q t) -> p q j t", t=PACK)[:, :, :, t0:t1],
             )
             cols = slice(b * PASS + t0 * P, b * PASS + t1 * P)
-            nc.vector.quantize_mx(out=w1_codes[:, cols].bitcast(FP8X4), scales=w1_plane[:, cols], in_=rounded[:])
+            nc.vector.quantize_mx(out=w1_codes[:, cols].bitcast(FP8X4), scales=w1_plane[:, cols], in_=rounded)
 
-        quantise_w1(0, 0, 1)
-        nc.scalar.mul(factor_s[:], factor_s[:], -2.0 / 3.0)
+        quantise_w1(0, 0, 2, curves[1][:, 0:BANK].bitcast(BF16), nc.scalar.copy)
+        quantise_w1(0, 2, 4, curves[1][:, BANK:S].bitcast(BF16), nc.vector.tensor_copy)
+
+        def row(k):
+            return picked[k // PACK][:, k % PACK, :]
 
         def features(k):
             cols = slice(k * P, (k + 1) * P)
-            curve = ring.tile([P, S], F32, name="curve")
-            feat = ring.tile([P, S], F32, name="feat")
+            curve = curves[k % 2]
+            feat = feats[k % 2]
             for s0 in range(0, S, BANK):
                 span = slice(s0, s0 + BANK)
                 gate = psum.tile([P, BANK], F32, name="gate", tag="bank")
@@ -127,27 +132,35 @@ def tile_list_rework_pad_scores_kernel(
                     out=gate[:], lhsT=w2_codes[:, 2 * k * P : 2 * (k + 1) * P].bitcast(FP4X4), lhsT_scale=w2_plane[:, cols],
                     rhs=v_codes[:, span].bitcast(FP8X4), rhs_scale=v_plane[:, span], start=True, stop=True,
                 )
+                nc.scalar.activation(curve[:, span], gate[:], ACT.Tanh, bias=shift[:], scale=0.5)
+                nc.scalar.activation(curve[:, span], curve[:, span], ACT.Copy, bias=4.0 / 3.0, scale=-2.0 / 3.0)
+            for s0 in range(0, S, BANK):
+                span = slice(s0, s0 + BANK)
                 lin = psum.tile([P, BANK], F32, name="lin", tag="bank")
                 nc.tensor.matmul_mx(
                     out=lin[:], lhsT=w1_codes[:, cols].bitcast(FP8X4), lhsT_scale=w1_plane[:, cols],
                     rhs=v_codes[:, span].bitcast(FP8X4), rhs_scale=v_plane[:, span], start=True, stop=True,
                 )
-                nc.scalar.activation(curve[:, span], gate[:], ACT.Tanh, bias=shift[:], scale=0.5)
-                nc.vector.scalar_tensor_tensor(feat[:, span], curve[:, span], -2.0, lin[:], ALU.add, ALU.mult)
-            return feat
+                if k == 0:
+                    nc.vector.tensor_tensor(curve[:, span], curve[:, span], factor_s[:, span], ALU.mult)
+                    nc.vector.tensor_tensor(feat[:, span], curve[:, span], lin[:], ALU.mult)
+                else:
+                    nc.scalar.copy(row(k - 1)[:, span], lin[:])
+            if k > 0:
+                nc.gpsimd.tensor_tensor(curve[:], curve[:], factor_s[:], ALU.mult)
+                nc.gpsimd.tensor_tensor(feat[:], curve[:], row(k - 1), ALU.mult)
 
-        def put(k, feat):
+        def put(k):
+            feat = feats[k % 2]
             width = BANK if k == 0 else S
             for s0 in range(0, S, width):
                 entries = idx2[:, s0 // LIST : (s0 + width) // LIST]
-                nc.vector.tensor_tensor(
-                    pages[k % 2][:].indirect(entries), feat[:, s0 : s0 + width], factor_s[:, s0 : s0 + width], ALU.mult
-                )
+                nc.vector.tensor_copy(out=pages[k % 2][:].indirect(entries), in_=feat[:, s0 : s0 + width])
 
-        def pick(k, picked, m0, width):
+        def pick(k, m0, width):
             entries = idx3[:, m0 // LIST : (m0 + width) // LIST]
             nc.vector.tensor_tensor(
-                picked[:, k % PACK, m0 : m0 + width], pages[k % 2][:].indirect(entries), factor_t[:, m0 : m0 + width], ALU.mult
+                row(k)[:, m0 : m0 + width], pages[k % 2][:].indirect(entries), factor_t[:, m0 : m0 + width], ALU.mult
             )
 
         z_codes = [keep.tile([P, M], U32, name="z_codes%d" % b, align_bytes=64) for b in range(PASSES)]
@@ -155,20 +168,21 @@ def tile_list_rework_pad_scores_kernel(
         mag_codes = [keep.tile([P, M], U32, name="mag_codes%d" % b, align_bytes=64) for b in range(PASSES)]
         mag_plane = [keep.tile([P, M], U8, name="mag_plane%d" % b, align_bytes=64) for b in range(PASSES)]
 
-        def add_paste(picked, offset, m0):
-            z = ring.tile([P, CHUNK * PACK], BF16, name="z", bufs=4, align_bytes=64)
-            mag = ring.tile([P, CHUNK * PACK], BF16, name="mag", bufs=4, align_bytes=64)
+        def add_paste(b, offset, m0):
+            half = slice(m0 // CHUNK % 2 * BANK, (m0 // CHUNK % 2 + 1) * BANK)
+            z = curves[1][:, half].bitcast(BF16)
+            mag = curves[0][:, half].bitcast(BF16)
             nc.vector.tensor_tensor(
-                z[:].rearrange("p (c i t) -> p c t i", i=4, t=PACK),
-                picked[:, :, m0 : m0 + CHUNK].rearrange("p t (c i) -> p c t i", i=4),
+                z.rearrange("p (c i t) -> p c t i", i=4, t=PACK),
+                picked[b][:, :, m0 : m0 + CHUNK].rearrange("p t (c i) -> p c t i", i=4),
                 offset[:, :, m0 : m0 + CHUNK].rearrange("p t (c i) -> p c t i", i=4),
                 ALU.add,
             )
-            nc.scalar.activation(mag[:], z[:], ACT.Abs)
+            nc.scalar.activation(mag, z, ACT.Abs)
             return z, mag
 
         def quantise(values, codes, plane, m0):
-            nc.vector.quantize_mx(out=codes[:, m0 : m0 + CHUNK].bitcast(FP8X4), scales=plane[:, m0 : m0 + CHUNK], in_=values[:])
+            nc.vector.quantize_mx(out=codes[:, m0 : m0 + CHUNK].bitcast(FP8X4), scales=plane[:, m0 : m0 + CHUNK], in_=values)
 
         def load_paste(b):
             offset = ring.tile([P, PACK, M], F32, name="offset", tag="wide")
@@ -184,75 +198,79 @@ def tile_list_rework_pad_scores_kernel(
             return raw
 
         def quantise_w4(b, raw):
-            half = N // 2
-            for n0 in range(0, N, half):
-                rounded = ring.tile([P, half * PACK], BF16, name="w4_rounded", tag="rounded", align_bytes=64)
+            for n0 in range(0, N, CHUNK):
+                side = (b * N + n0) // CHUNK % 2
+                rounded = feats[0][:, side * BANK : (side + 1) * BANK].bitcast(BF16)
                 nc.scalar.copy(
-                    out=rounded[:].rearrange("p (c i j) -> p c j i", i=4, j=PACK),
-                    in_=raw[:, :, n0 : n0 + half].rearrange("p j (c i) -> p c j i", i=4),
+                    out=rounded.rearrange("p (c i j) -> p c j i", i=4, j=PACK),
+                    in_=raw[:, :, n0 : n0 + CHUNK].rearrange("p j (c i) -> p c j i", i=4),
                 )
-                cols = slice(b * N + n0, b * N + n0 + half)
-                nc.vector.quantize_mx(out=w4_codes[:, cols].bitcast(FP8X4), scales=w4_plane[:, cols], in_=rounded[:])
+                cols = slice(b * N + n0, b * N + n0 + CHUNK)
+                nc.vector.quantize_mx(out=w4_codes[:, cols].bitcast(FP8X4), scales=w4_plane[:, cols], in_=rounded)
 
         w3_codes = keep.tile([P, PASSES, 2 * N], U8, name="w3_codes", align_bytes=64)
 
-        def finish_pass(b, picked, offset, last_tile):
-            waiting = None
-            for m0 in range(0, M, CHUNK):
-                if last_tile is not None:
-                    pick(last_tile, picked, m0, CHUNK)
-                z, mag = add_paste(picked, offset, m0)
-                if waiting is not None:
-                    quantise(waiting[0], mag_codes[b], mag_plane[b], waiting[1])
-                quantise(z, z_codes[b], z_plane[b], m0)
-                waiting = (mag, m0)
-            quantise(waiting[0], mag_codes[b], mag_plane[b], waiting[1])
+        def scores(m0):
+            span = slice(m0, m0 + CHUNK)
+            for n0 in range(0, N, 2 * P):
+                signed = psum.tile([P, 2, CHUNK], F32, name="signed", tag="bank")
+                sized = psum.tile([P, 2, CHUNK], F32, name="sized", tag="bank")
+                for b in range(PASSES):
+                    for u in range(2):
+                        n = n0 + u * P
+                        nc.tensor.matmul_mx(
+                            out=signed[:, u, :], lhsT=w3_codes[:, b, 2 * n : 2 * (n + P)].bitcast(FP4X4), lhsT_scale=w3_plane[:, b, n : n + P],
+                            rhs=z_codes[b][:, span].bitcast(FP8X4), rhs_scale=z_plane[b][:, span],
+                            start=(b == 0 and u == 0), stop=(b == PASSES - 1 and u == 1),
+                        )
+                for b in range(PASSES):
+                    for u in range(2):
+                        cols = slice(b * N + n0 + u * P, b * N + n0 + (u + 1) * P)
+                        nc.tensor.matmul_mx(
+                            out=sized[:, u, :], lhsT=w4_codes[:, cols].bitcast(FP8X4), lhsT_scale=w4_plane[:, cols],
+                            rhs=mag_codes[b][:, span].bitcast(FP8X4), rhs_scale=mag_plane[b][:, span],
+                            start=(b == 0 and u == 0), stop=(b == PASSES - 1 and u == 1),
+                        )
+                bounded = ring.tile([P, 2, CHUNK], F32, name="bounded", bufs=3)
+                nc.scalar.activation(bounded[:], signed[:], ACT.Tanh)
+                score = ring.tile([P, 2, CHUNK], F32, name="score", bufs=4)
+                nc.vector.tensor_tensor(score[:], bounded[:], sized[:], ALU.add)
+                nc.sync.dma_start(out=out[n0 : n0 + 2 * P, span].rearrange("(u p) m -> p u m", u=2), in_=score[:])
 
-        feats = {0: features(0)}
-        quantise_w1(0, 1, PACK)
+        def finish_pass(b, offset):
+            last = b == PASSES - 1
+            mags = {}
+            for m0 in range(0, M, CHUNK):
+                if last:
+                    pick(ROW_TILES - 1, m0, CHUNK)
+                z, mags[m0] = add_paste(b, offset, m0)
+                if m0 > 0:
+                    quantise(mags[m0 - CHUNK], mag_codes[b], mag_plane[b], m0 - CHUNK)
+                quantise(z, z_codes[b], z_plane[b], m0)
+                if last and m0 >= 2 * CHUNK:
+                    scores(m0 - 2 * CHUNK)
+            quantise(mags[M - CHUNK], mag_codes[b], mag_plane[b], M - CHUNK)
+
+        features(0)
         offsets = [load_paste(0)]
-        picked = {}
-        w4_raw = {}
-        for k in range(ROW_TILES):
-            if k + 1 < ROW_TILES:
-                feats[k + 1] = features(k + 1)
-            put(k, feats[k])
+        for k in range(ROW_TILES - 1):
+            features(k + 1)
+            put(k)
             if k == 0:
-                quantise_w1(1, 0, PACK)
                 offsets.append(load_paste(1))
-                w4_raw[0] = load_w4(0)
-                w4_raw[1] = load_w4(1)
+                w4_raw = [load_w4(b) for b in range(PASSES)]
                 nc.sync.dma_start(out=w3_codes[:].bitcast(I32), in_=w3_words.rearrange("a p c -> p a c").bitcast(I32))
                 load_scale_rows(nc.sync, w3_plane[:], w3_scales)
+            if k == 1:
+                rounded = ring.tile([P, PASS * PACK], BF16, name="w1_rounded", bufs=1, align_bytes=64)
+                quantise_w1(1, 0, PACK, rounded[:], nc.scalar.copy)
             if k >= 1:
-                j = k - 1
-                if j % PACK == 0:
-                    picked[j // PACK] = keep.tile([P, PACK, M], F32, name="picked")
-                pick(j, picked[j // PACK], 0, M)
-                if j == PACK - 1:
-                    finish_pass(0, picked[0], offsets[0], None)
-            if k in (2, 3):
-                quantise_w4(k - 2, w4_raw[k - 2])
-        finish_pass(1, picked[1], offsets[1], ROW_TILES - 1)
-
-        for m0 in range(0, M, BANK):
-            span = slice(m0, m0 + BANK)
-            for n0 in range(0, N, P):
-                signed = psum.tile([P, BANK], F32, name="signed", tag="bank")
-                sized = psum.tile([P, BANK], F32, name="sized", tag="bank")
-                for b in range(PASSES):
-                    nc.tensor.matmul_mx(
-                        out=signed[:], lhsT=w3_codes[:, b, 2 * n0 : 2 * (n0 + P)].bitcast(FP4X4), lhsT_scale=w3_plane[:, b, n0 : n0 + P],
-                        rhs=z_codes[b][:, span].bitcast(FP8X4), rhs_scale=z_plane[b][:, span], start=(b == 0), stop=(b == PASSES - 1),
-                    )
-                for b in range(PASSES):
-                    cols = slice(b * N + n0, b * N + n0 + P)
-                    nc.tensor.matmul_mx(
-                        out=sized[:], lhsT=w4_codes[:, cols].bitcast(FP8X4), lhsT_scale=w4_plane[:, cols],
-                        rhs=mag_codes[b][:, span].bitcast(FP8X4), rhs_scale=mag_plane[b][:, span], start=(b == 0), stop=(b == PASSES - 1),
-                    )
-                bounded = ring.tile([P, BANK], F32, name="bounded", bufs=3)
-                nc.scalar.activation(bounded[:], signed[:], ACT.Tanh)
-                score = ring.tile([P, BANK], F32, name="score", bufs=4)
-                nc.vector.tensor_tensor(score[:], bounded[:], sized[:], ALU.add)
-                nc.sync.dma_start(out=out[n0 : n0 + P, span], in_=score[:])
+                pick(k - 1, 0, M)
+        finish_pass(0, offsets[0])
+        for b in range(PASSES):
+            quantise_w4(b, w4_raw[b])
+        pick(ROW_TILES - 2, 0, M)
+        put(ROW_TILES - 1)
+        finish_pass(1, offsets[1])
+        scores(M - 2 * CHUNK)
+        scores(M - CHUNK)

@@ -2,6 +2,7 @@ import math
 from contextlib import ExitStack
 
 import concourse.mybir as mybir
+from concourse.masks import make_identity
 
 K, H, N, T, S, M, T2 = 512, 1024, 768, 4096, 1024, 1024, 2048
 FLOPS = 2 * (2 * K * H * S + 2 * H * N * M)
@@ -25,6 +26,7 @@ ROW_TILES = H // P
 BANK = 512
 CHUNK = 256
 LIST = 16
+PIECES = (slice(0, 336), slice(336, 688), slice(688, 1024))
 
 
 def tile_list_rework_pad_scores_kernel(
@@ -57,6 +59,8 @@ def tile_list_rework_pad_scores_kernel(
         for page in pages:
             nc.gpsimd.memset(page[:], 0.0)
         nc.gpsimd.memset(w3_plane[:].bitcast(I32), 0)
+        identity = keep.tile([P, P], F32, name="identity")
+        make_identity(nc, identity[:])
         shift = keep.tile([P, 1], F32, name="shift")
         nc.vector.memset(shift[:], 1.0)
         nc.vector.tensor_scalar(shift[:], shift[:], 0.5 * math.log(3.0), None, ALU.mult)
@@ -85,8 +89,8 @@ def tile_list_rework_pad_scores_kernel(
         w2_codes = keep.tile([P, 2 * H], U8, name="w2_codes", align_bytes=64)
         w2_plane = keep.tile([P, H], U8, name="w2_plane", align_bytes=64)
         nc.vector.tensor_copy(
-            out=w2_codes[:].rearrange("p (b t q e) -> p b t q e", b=PASSES, t=PACK, e=2),
-            in_=w2_raw[:].rearrange("p (b q t e) -> p b t q e", b=PASSES, t=PACK, e=2),
+            out=w2_codes[:].bitcast(U16).rearrange("p (b t q) -> p b t q", b=PASSES, t=PACK),
+            in_=w2_raw[:].bitcast(U16).rearrange("p (b q t) -> p b t q", b=PASSES, t=PACK),
         )
         nc.vector.tensor_copy(
             out=w2_plane[:].rearrange("p (b t q) -> p b t q", b=PASSES, t=PACK),
@@ -115,8 +119,8 @@ def tile_list_rework_pad_scores_kernel(
             cols = slice(b * PASS + t0 * P, b * PASS + t1 * P)
             nc.vector.quantize_mx(out=w1_codes[:, cols].bitcast(FP8X4), scales=w1_plane[:, cols], in_=rounded)
 
-        quantise_w1(0, 0, 2, curves[1][:, 0:BANK].bitcast(BF16), nc.scalar.copy)
-        quantise_w1(0, 2, 4, curves[1][:, BANK:S].bitcast(BF16), nc.vector.tensor_copy)
+        quantise_w1(0, 0, 2, curves[1][:, 0:BANK].bitcast(BF16), nc.vector.tensor_copy)
+        quantise_w1(0, 2, 4, curves[1][:, BANK:S].bitcast(BF16), nc.scalar.copy)
 
         def row(k):
             return picked[k // PACK][:, k % PACK, :]
@@ -147,8 +151,10 @@ def tile_list_rework_pad_scores_kernel(
                 else:
                     nc.scalar.copy(row(k - 1)[:, span], lin[:])
             if k > 0:
-                nc.gpsimd.tensor_tensor(curve[:], curve[:], factor_s[:], ALU.mult)
-                nc.gpsimd.tensor_tensor(feat[:], curve[:], row(k - 1), ALU.mult)
+                for piece in PIECES:
+                    nc.gpsimd.tensor_tensor(curve[:, piece], curve[:, piece], factor_s[:, piece], ALU.mult)
+                for piece in PIECES:
+                    nc.gpsimd.tensor_tensor(feat[:, piece], curve[:, piece], row(k - 1)[:, piece], ALU.mult)
 
         def put(k):
             feat = feats[k % 2]
@@ -168,21 +174,48 @@ def tile_list_rework_pad_scores_kernel(
         mag_codes = [keep.tile([P, M], U32, name="mag_codes%d" % b, align_bytes=64) for b in range(PASSES)]
         mag_plane = [keep.tile([P, M], U8, name="mag_plane%d" % b, align_bytes=64) for b in range(PASSES)]
 
+        z = keep.tile([P, M * PACK], BF16, name="z", align_bytes=64)
+        mag = keep.tile([P, M * PACK], BF16, name="mag", align_bytes=64)
+
+        def add_paste_turned(offset, m0):
+            side = m0 // CHUNK % 2
+            pairs = curves[m0 // BANK][:, side * BANK : (side + 1) * BANK].rearrange("m (u g p) -> m u g p", u=2, g=2)
+            for u in range(2):
+                total = psum.tile([P, 2, 2, P], F32, name="total", tag="bank")
+                for g in range(2):
+                    cols = slice(m0 + g * P, m0 + (g + 1) * P)
+                    for e in range(2):
+                        t = 2 * u + e
+                        nc.tensor.matmul(total[:, g, e, :], row(t)[:, cols], identity[:], start=True, stop=False, is_transpose=True)
+                        nc.tensor.matmul(total[:, g, e, :], offset[:, t, cols], identity[:], start=False, stop=True, is_transpose=True)
+                nc.scalar.copy(
+                    out=pairs[:, u].rearrange("m g p -> m (g p)").bitcast(BF16).rearrange("m (g p e) -> m g p e", g=2, e=2),
+                    in_=total[:].rearrange("m g e p -> m g p e"),
+                )
+            back = psum.tile([P, 2, 2, P], F32, name="back", tag="bank")
+            for g in range(2):
+                for u in range(2):
+                    nc.tensor.transpose(back[:, g, u, :], pairs[:, u, g, :], identity[:])
+            nc.scalar.copy(
+                out=chunk(z, m0).bitcast(F32).rearrange("p (g m u) -> p g m u", g=2, u=2), in_=back[:].rearrange("p g u m -> p g m u")
+            )
+
+        def chunk(values, m0):
+            return values[:, m0 * PACK : (m0 + CHUNK) * PACK]
+
         def add_paste(b, offset, m0):
-            half = slice(m0 // CHUNK % 2 * BANK, (m0 // CHUNK % 2 + 1) * BANK)
-            z = curves[1][:, half].bitcast(BF16)
-            mag = curves[0][:, half].bitcast(BF16)
             nc.vector.tensor_tensor(
-                z.rearrange("p (c i t) -> p c t i", i=4, t=PACK),
+                chunk(z, m0).rearrange("p (c i t) -> p c t i", i=4, t=PACK),
                 picked[b][:, :, m0 : m0 + CHUNK].rearrange("p t (c i) -> p c t i", i=4),
                 offset[:, :, m0 : m0 + CHUNK].rearrange("p t (c i) -> p c t i", i=4),
                 ALU.add,
             )
-            nc.scalar.activation(mag, z, ACT.Abs)
-            return z, mag
 
-        def quantise(values, codes, plane, m0):
-            nc.vector.quantize_mx(out=codes[:, m0 : m0 + CHUNK].bitcast(FP8X4), scales=plane[:, m0 : m0 + CHUNK], in_=values)
+        def magnitude(m0):
+            nc.scalar.activation(chunk(mag, m0), chunk(z, m0), ACT.Abs)
+
+        def quantise(values, codes, plane, c0, c1):
+            nc.vector.quantize_mx(out=codes[:, c0:c1].bitcast(FP8X4), scales=plane[:, c0:c1], in_=values[:, c0 * PACK : c1 * PACK])
 
         def load_paste(b):
             offset = ring.tile([P, PACK, M], F32, name="offset", tag="wide")
@@ -197,16 +230,13 @@ def tile_list_rework_pad_scores_kernel(
             nc.sync.dma_start(out=raw[:], in_=w4[b * PASS : (b + 1) * PASS, :].rearrange("(p j) n -> p j n", j=PACK))
             return raw
 
-        def quantise_w4(b, raw):
-            for n0 in range(0, N, CHUNK):
-                side = (b * N + n0) // CHUNK % 2
-                rounded = feats[0][:, side * BANK : (side + 1) * BANK].bitcast(BF16)
-                nc.scalar.copy(
-                    out=rounded.rearrange("p (c i j) -> p c j i", i=4, j=PACK),
-                    in_=raw[:, :, n0 : n0 + CHUNK].rearrange("p j (c i) -> p c j i", i=4),
-                )
-                cols = slice(b * N + n0, b * N + n0 + CHUNK)
-                nc.vector.quantize_mx(out=w4_codes[:, cols].bitcast(FP8X4), scales=w4_plane[:, cols], in_=rounded)
+        w4_rounded = keep.tile([P, PASSES * N * PACK], BF16, name="w4_rounded", align_bytes=64)
+
+        def round_w4(b, raw):
+            nc.scalar.copy(
+                out=w4_rounded[:, b * N * PACK : (b + 1) * N * PACK].rearrange("p (c i j) -> p c j i", i=4, j=PACK),
+                in_=raw[:].rearrange("p j (c i) -> p c j i", i=4),
+            )
 
         w3_codes = keep.tile([P, PASSES, 2 * N], U8, name="w3_codes", align_bytes=64)
 
@@ -237,20 +267,6 @@ def tile_list_rework_pad_scores_kernel(
                 nc.vector.tensor_tensor(score[:], bounded[:], sized[:], ALU.add)
                 nc.sync.dma_start(out=out[n0 : n0 + 2 * P, span].rearrange("(u p) m -> p u m", u=2), in_=score[:])
 
-        def finish_pass(b, offset):
-            last = b == PASSES - 1
-            mags = {}
-            for m0 in range(0, M, CHUNK):
-                if last:
-                    pick(ROW_TILES - 1, m0, CHUNK)
-                z, mags[m0] = add_paste(b, offset, m0)
-                if m0 > 0:
-                    quantise(mags[m0 - CHUNK], mag_codes[b], mag_plane[b], m0 - CHUNK)
-                quantise(z, z_codes[b], z_plane[b], m0)
-                if last and m0 >= 2 * CHUNK:
-                    scores(m0 - 2 * CHUNK)
-            quantise(mags[M - CHUNK], mag_codes[b], mag_plane[b], M - CHUNK)
-
         features(0)
         offsets = [load_paste(0)]
         for k in range(ROW_TILES - 1):
@@ -266,11 +282,27 @@ def tile_list_rework_pad_scores_kernel(
                 quantise_w1(1, 0, PACK, rounded[:], nc.scalar.copy)
             if k >= 1:
                 pick(k - 1, 0, M)
-        finish_pass(0, offsets[0])
-        for b in range(PASSES):
-            quantise_w4(b, w4_raw[b])
+            if k in (2, 3):
+                round_w4(k - 2, w4_raw[k - 2])
+            if k == 3:
+                quantise(w4_rounded, w4_codes, w4_plane, 0, 1024)
+                quantise(w4_rounded, w4_codes, w4_plane, 1024, PASSES * N)
+        for m0 in range(0, M, CHUNK):
+            add_paste_turned(offsets[0], m0)
+            magnitude(m0)
+        quantise(z, z_codes[0], z_plane[0], 0, M)
+        quantise(mag, mag_codes[0], mag_plane[0], 0, M)
         pick(ROW_TILES - 2, 0, M)
         put(ROW_TILES - 1)
-        finish_pass(1, offsets[1])
+        for m0 in range(0, M, CHUNK):
+            pick(ROW_TILES - 1, m0, CHUNK)
+            add_paste(1, offsets[1], m0)
+            magnitude(m0)
+            if m0 > 0:
+                quantise(mag, mag_codes[1], mag_plane[1], m0 - CHUNK, m0)
+            quantise(z, z_codes[1], z_plane[1], m0, m0 + CHUNK)
+            if m0 >= 2 * CHUNK:
+                scores(m0 - 2 * CHUNK)
+        quantise(mag, mag_codes[1], mag_plane[1], M - CHUNK, M)
         scores(M - 2 * CHUNK)
         scores(M - CHUNK)

@@ -23,10 +23,12 @@ PACK = 4
 PASS = P * PACK
 PASSES = H // PASS
 ROW_TILES = H // P
+LAST = ROW_TILES - 1
 BANK = 512
 CHUNK = 256
 LIST = 16
-PIECES = (slice(0, 336), slice(336, 688), slice(688, 1024))
+LINE = 4
+QUANT_MAX = 1024
 
 
 def tile_list_rework_pad_scores_kernel(
@@ -43,11 +45,11 @@ def tile_list_rework_pad_scores_kernel(
         idx2 = lists.tile([P, S // LIST], U16, name="idx2")
         idx3 = lists.tile([P, M // LIST], U16, name="idx3")
 
-        def load_scale_rows(queue, plane, rows):
-            for q in range(4):
-                queue.dma_start(
-                    out=plane[32 * q : 32 * q + 4].bitcast(I32),
-                    in_=rows[:, 4 * q : 4 * q + 4, :].rearrange("a r c -> r a c").bitcast(I32),
+        def load_scale_rows(plane, rows):
+            for quadrant in range(4):
+                nc.sync.dma_start(
+                    out=plane[32 * quadrant : 32 * quadrant + 4].bitcast(I32),
+                    in_=rows[:, 4 * quadrant : 4 * quadrant + 4, :].rearrange("a r c -> r a c").bitcast(I32),
                 )
 
         tab_plane = keep.tile([P, T], U8, name="tab_plane", align_bytes=64)
@@ -57,34 +59,34 @@ def tile_list_rework_pad_scores_kernel(
         nc.gpsimd.memset(w2_plane_raw[:].bitcast(I32), 0)
         pages = [keep.tile([P, T2], F32, name="page%d" % n) for n in range(2)]
         for page in pages:
-            nc.gpsimd.memset(page[:], 0.0)
+            nc.vector.memset(page[:], 0.0)
         nc.gpsimd.memset(w3_plane[:].bitcast(I32), 0)
         identity = keep.tile([P, P], F32, name="identity")
         make_identity(nc, identity[:])
-        shift = keep.tile([P, 1], F32, name="shift")
-        nc.vector.memset(shift[:], 1.0)
-        nc.vector.tensor_scalar(shift[:], shift[:], 0.5 * math.log(3.0), None, ALU.mult)
+        half_ln3 = keep.tile([P, 1], F32, name="half_ln3")
+        nc.vector.memset(half_ln3[:], 1.0)
+        nc.vector.tensor_scalar(half_ln3[:], half_ln3[:], 0.5 * math.log(3.0), None, ALU.mult)
 
         nc.sync.dma_start(idx[:], offs)
         w2_raw = keep.tile([P, 2 * H], U8, name="w2_raw")
         nc.sync.dma_start(out=w2_raw[:].bitcast(I32), in_=w2_words[0].bitcast(I32))
-        load_scale_rows(nc.sync, tab_plane[:].rearrange("p (a t) -> p a t", a=1), tab_scales)
+        load_scale_rows(tab_plane[:].rearrange("p (a t) -> p a t", a=1), tab_scales)
         tab = ring.tile([P, T], I32, name="tab", tag="wide")
         nc.sync.dma_start(out=tab[:], in_=tab_words[0].rearrange("p t i -> p (t i)").bitcast(I32))
-        load_scale_rows(nc.sync, w2_plane_raw[:], w2_scales)
+        load_scale_rows(w2_plane_raw[:], w2_scales)
         w1_rows = w1.rearrange("(p j) r -> p j r", j=PACK)
         w1_raw = []
-        factor_s = keep.tile([P, S], F32, name="factor_s")
-        factor_t = keep.tile([P, M], F32, name="factor_t")
+        put_factor = keep.tile([P, S], F32, name="put_factor")
+        pick_factor = keep.tile([P, M], F32, name="pick_factor")
         for b in range(PASSES):
             raw = ring.tile([P, PACK, PASS], F32, name="w1_raw", tag="raw")
             nc.sync.dma_start(out=raw[:], in_=w1_rows[:, :, b * PASS : (b + 1) * PASS])
             w1_raw.append(raw)
             if b == 0:
                 nc.sync.dma_start(idx2[:], offs2)
-                nc.sync.dma_start(out=factor_s[:], in_=wgs)
+                nc.sync.dma_start(out=put_factor[:], in_=wgs)
         nc.sync.dma_start(idx3[:], offs3)
-        nc.sync.dma_start(out=factor_t[:], in_=wgt)
+        nc.sync.dma_start(out=pick_factor[:], in_=wgt)
 
         w2_codes = keep.tile([P, 2 * H], U8, name="w2_codes", align_bytes=64)
         w2_plane = keep.tile([P, H], U8, name="w2_plane", align_bytes=64)
@@ -109,7 +111,7 @@ def tile_list_rework_pad_scores_kernel(
 
         curves = [keep.tile([P, S], F32, name="curve%d" % n, align_bytes=64) for n in range(2)]
         feats = [keep.tile([P, S], F32, name="feat%d" % n, align_bytes=64) for n in range(2)]
-        picked = [keep.tile([P, PACK, M], F32, name="picked%d" % b) for b in range(PASSES)]
+        picked = [keep.tile([P, PACK, M], F32, name="picked%d" % b, align_bytes=64) for b in range(PASSES)]
 
         def quantise_w1(b, t0, t1, rounded, copy):
             copy(
@@ -119,8 +121,11 @@ def tile_list_rework_pad_scores_kernel(
             cols = slice(b * PASS + t0 * P, b * PASS + t1 * P)
             nc.vector.quantize_mx(out=w1_codes[:, cols].bitcast(FP8X4), scales=w1_plane[:, cols], in_=rounded)
 
-        quantise_w1(0, 0, 2, curves[1][:, 0:BANK].bitcast(BF16), nc.vector.tensor_copy)
-        quantise_w1(0, 2, 4, curves[1][:, BANK:S].bitcast(BF16), nc.scalar.copy)
+        first = ring.tile([P, P * PACK], BF16, name="w1_first", bufs=1, align_bytes=64)
+        quantise_w1(0, 0, 1, first[:], nc.vector.tensor_copy)
+        rounded = ring.tile([P, (PACK - 1) * P * PACK], BF16, name="w1_rounded", bufs=1, align_bytes=64)
+        quantise_w1(0, 1, PACK, rounded[:], nc.scalar.copy)
+        nc.vector.tensor_scalar(put_factor[:], put_factor[:], -2.0 / 3.0, None, ALU.mult)
 
         def row(k):
             return picked[k // PACK][:, k % PACK, :]
@@ -136,8 +141,7 @@ def tile_list_rework_pad_scores_kernel(
                     out=gate[:], lhsT=w2_codes[:, 2 * k * P : 2 * (k + 1) * P].bitcast(FP4X4), lhsT_scale=w2_plane[:, cols],
                     rhs=v_codes[:, span].bitcast(FP8X4), rhs_scale=v_plane[:, span], start=True, stop=True,
                 )
-                nc.scalar.activation(curve[:, span], gate[:], ACT.Tanh, bias=shift[:], scale=0.5)
-                nc.scalar.activation(curve[:, span], curve[:, span], ACT.Copy, bias=4.0 / 3.0, scale=-2.0 / 3.0)
+                nc.scalar.activation(curve[:, span], gate[:], ACT.Tanh, bias=half_ln3[:], scale=0.5)
             for s0 in range(0, S, BANK):
                 span = slice(s0, s0 + BANK)
                 lin = psum.tile([P, BANK], F32, name="lin", tag="bank")
@@ -145,28 +149,21 @@ def tile_list_rework_pad_scores_kernel(
                     out=lin[:], lhsT=w1_codes[:, cols].bitcast(FP8X4), lhsT_scale=w1_plane[:, cols],
                     rhs=v_codes[:, span].bitcast(FP8X4), rhs_scale=v_plane[:, span], start=True, stop=True,
                 )
-                if k == 0:
-                    nc.vector.tensor_tensor(curve[:, span], curve[:, span], factor_s[:, span], ALU.mult)
-                    nc.vector.tensor_tensor(feat[:, span], curve[:, span], lin[:], ALU.mult)
-                else:
-                    nc.scalar.copy(row(k - 1)[:, span], lin[:])
-            if k > 0:
-                for piece in PIECES:
-                    nc.gpsimd.tensor_tensor(curve[:, piece], curve[:, piece], factor_s[:, piece], ALU.mult)
-                for piece in PIECES:
-                    nc.gpsimd.tensor_tensor(feat[:, piece], curve[:, piece], row(k - 1)[:, piece], ALU.mult)
+                nc.vector.scalar_tensor_tensor(feat[:, span], curve[:, span], -2.0, lin[:], ALU.add, ALU.mult)
 
         def put(k):
             feat = feats[k % 2]
             width = BANK if k == 0 else S
             for s0 in range(0, S, width):
                 entries = idx2[:, s0 // LIST : (s0 + width) // LIST]
-                nc.vector.tensor_copy(out=pages[k % 2][:].indirect(entries), in_=feat[:, s0 : s0 + width])
+                nc.vector.tensor_tensor(
+                    pages[k % 2][:].indirect(entries), feat[:, s0 : s0 + width], put_factor[:, s0 : s0 + width], ALU.mult
+                )
 
         def pick(k, m0, width):
             entries = idx3[:, m0 // LIST : (m0 + width) // LIST]
             nc.vector.tensor_tensor(
-                row(k)[:, m0 : m0 + width], pages[k % 2][:].indirect(entries), factor_t[:, m0 : m0 + width], ALU.mult
+                row(k)[:, m0 : m0 + width], pages[k % 2][:].indirect(entries), pick_factor[:, m0 : m0 + width], ALU.mult
             )
 
         z_codes = [keep.tile([P, M], U32, name="z_codes%d" % b, align_bytes=64) for b in range(PASSES)]
@@ -177,50 +174,46 @@ def tile_list_rework_pad_scores_kernel(
         z = keep.tile([P, M * PACK], BF16, name="z", align_bytes=64)
         mag = keep.tile([P, M * PACK], BF16, name="mag", align_bytes=64)
 
-        def add_paste_turned(offset, m0):
-            side = m0 // CHUNK % 2
-            pairs = curves[m0 // BANK][:, side * BANK : (side + 1) * BANK].rearrange("m (u g p) -> m u g p", u=2, g=2)
-            for u in range(2):
-                total = psum.tile([P, 2, 2, P], F32, name="total", tag="bank")
-                for g in range(2):
-                    cols = slice(m0 + g * P, m0 + (g + 1) * P)
-                    for e in range(2):
-                        t = 2 * u + e
-                        nc.tensor.matmul(total[:, g, e, :], row(t)[:, cols], identity[:], start=True, stop=False, is_transpose=True)
-                        nc.tensor.matmul(total[:, g, e, :], offset[:, t, cols], identity[:], start=False, stop=True, is_transpose=True)
-                nc.scalar.copy(
-                    out=pairs[:, u].rearrange("m g p -> m (g p)").bitcast(BF16).rearrange("m (g p e) -> m g p e", g=2, e=2),
-                    in_=total[:].rearrange("m g e p -> m g p e"),
-                )
-            back = psum.tile([P, 2, 2, P], F32, name="back", tag="bank")
-            for g in range(2):
-                for u in range(2):
-                    nc.tensor.transpose(back[:, g, u, :], pairs[:, u, g, :], identity[:])
-            nc.scalar.copy(
-                out=chunk(z, m0).bitcast(F32).rearrange("p (g m u) -> p g m u", g=2, u=2), in_=back[:].rearrange("p g u m -> p g m u")
-            )
-
         def chunk(values, m0):
             return values[:, m0 * PACK : (m0 + CHUNK) * PACK]
 
-        def add_paste(b, offset, m0):
+        def add_paste_turned(paste_rows, m0):
+            back = psum.tile([P, CHUNK // P, 2, P], F32, name="back", tag="bank")
+            for g in range(CHUNK // P):
+                cols = slice(m0 + g * P, m0 + (g + 1) * P)
+                total = psum.tile([P, PACK, P], F32, name="total", tag="bank")
+                for t in range(PACK):
+                    nc.tensor.matmul(total[:, t, :], row(t)[:, cols], identity[:], start=True, stop=False, is_transpose=True)
+                    nc.tensor.matmul(total[:, t, :], paste_rows[:, t, cols], identity[:], start=False, stop=True, is_transpose=True)
+                pairs = ring.tile([P, PACK * P], BF16, name="pairs", bufs=4)
+                nc.scalar.copy(
+                    out=pairs[:].rearrange("m (u p e) -> m u p e", u=2, e=2), in_=total[:].rearrange("m (u e) p -> m u p e", e=2)
+                )
+                for u in range(2):
+                    nc.tensor.transpose(back[:, g, u, :], pairs[:].bitcast(F32)[:, u * P : (u + 1) * P], identity[:])
+            nc.scalar.copy(
+                out=chunk(z, m0).bitcast(F32).rearrange("p (g m u) -> p g m u", g=CHUNK // P, u=2),
+                in_=back[:].rearrange("p g u m -> p g m u"),
+            )
+
+        def add_paste(paste_rows, m0):
             nc.vector.tensor_tensor(
-                chunk(z, m0).rearrange("p (c i t) -> p c t i", i=4, t=PACK),
-                picked[b][:, :, m0 : m0 + CHUNK].rearrange("p t (c i) -> p c t i", i=4),
-                offset[:, :, m0 : m0 + CHUNK].rearrange("p t (c i) -> p c t i", i=4),
+                chunk(z, m0).rearrange("p (c i t) -> p c t i", i=LINE, t=PACK),
+                picked[1][:, :, m0 : m0 + CHUNK].rearrange("p t (c i) -> p c t i", i=LINE),
+                paste_rows[:, :, m0 : m0 + CHUNK].rearrange("p t (c i) -> p c t i", i=LINE),
                 ALU.add,
             )
 
-        def magnitude(m0):
-            nc.scalar.activation(chunk(mag, m0), chunk(z, m0), ACT.Abs)
+        def magnitude(into, m0):
+            nc.scalar.activation(into, chunk(z, m0), ACT.Abs)
 
         def quantise(values, codes, plane, c0, c1):
             nc.vector.quantize_mx(out=codes[:, c0:c1].bitcast(FP8X4), scales=plane[:, c0:c1], in_=values[:, c0 * PACK : c1 * PACK])
 
         def load_paste(b):
-            offset = ring.tile([P, PACK, M], F32, name="offset", tag="wide")
-            nc.sync.dma_start(out=offset[:], in_=paste[b * PASS : (b + 1) * PASS, :].rearrange("(p t) m -> p t m", t=PACK))
-            return offset
+            paste_rows = ring.tile([P, PACK, M], F32, name="paste_rows", tag="wide")
+            nc.sync.dma_start(out=paste_rows[:], in_=paste[b * PASS : (b + 1) * PASS, :].rearrange("(p t) m -> p t m", t=PACK))
+            return paste_rows
 
         w4_codes = keep.tile([P, PASSES * N], U32, name="w4_codes", align_bytes=64)
         w4_plane = keep.tile([P, PASSES * N], U8, name="w4_plane", align_bytes=64)
@@ -234,8 +227,8 @@ def tile_list_rework_pad_scores_kernel(
 
         def round_w4(b, raw):
             nc.scalar.copy(
-                out=w4_rounded[:, b * N * PACK : (b + 1) * N * PACK].rearrange("p (c i j) -> p c j i", i=4, j=PACK),
-                in_=raw[:].rearrange("p j (c i) -> p c j i", i=4),
+                out=w4_rounded[:, b * N * PACK : (b + 1) * N * PACK].rearrange("p (c i j) -> p c j i", i=LINE, j=PACK),
+                in_=raw[:].rearrange("p j (c i) -> p c j i", i=LINE),
             )
 
         w3_codes = keep.tile([P, PASSES, 2 * N], U8, name="w3_codes", align_bytes=64)
@@ -268,36 +261,42 @@ def tile_list_rework_pad_scores_kernel(
                 nc.sync.dma_start(out=out[n0 : n0 + 2 * P, span].rearrange("(u p) m -> p u m", u=2), in_=score[:])
 
         features(0)
-        offsets = [load_paste(0)]
-        for k in range(ROW_TILES - 1):
+        paste_tiles = [load_paste(0)]
+        for k in range(LAST):
             features(k + 1)
             put(k)
             if k == 0:
-                offsets.append(load_paste(1))
+                paste_tiles.append(load_paste(1))
                 w4_raw = [load_w4(b) for b in range(PASSES)]
                 nc.sync.dma_start(out=w3_codes[:].bitcast(I32), in_=w3_words.rearrange("a p c -> p a c").bitcast(I32))
-                load_scale_rows(nc.sync, w3_plane[:], w3_scales)
+                load_scale_rows(w3_plane[:], w3_scales)
             if k == 1:
                 rounded = ring.tile([P, PASS * PACK], BF16, name="w1_rounded", bufs=1, align_bytes=64)
                 quantise_w1(1, 0, PACK, rounded[:], nc.scalar.copy)
-            if k >= 1:
+            if 1 <= k < LAST - 1:
                 pick(k - 1, 0, M)
-            if k in (2, 3):
+            if 2 <= k < 2 + PASSES:
                 round_w4(k - 2, w4_raw[k - 2])
-            if k == 3:
-                quantise(w4_rounded, w4_codes, w4_plane, 0, 1024)
-                quantise(w4_rounded, w4_codes, w4_plane, 1024, PASSES * N)
+            if k == 1 + PASSES:
+                quantise(w4_rounded, w4_codes, w4_plane, 0, QUANT_MAX)
+                quantise(w4_rounded, w4_codes, w4_plane, QUANT_MAX, PASSES * N)
+
+        borrowed = [row(k).bitcast(BF16) for k in (LAST, LAST - 2)]
         for m0 in range(0, M, CHUNK):
-            add_paste_turned(offsets[0], m0)
-            magnitude(m0)
+            add_paste_turned(paste_tiles[0], m0)
+            magnitude(chunk(borrowed[m0 // BANK], m0 % BANK), m0)
         quantise(z, z_codes[0], z_plane[0], 0, M)
-        quantise(mag, mag_codes[0], mag_plane[0], 0, M)
-        pick(ROW_TILES - 2, 0, M)
-        put(ROW_TILES - 1)
+        for half in range(2):
+            cols = slice(half * BANK, (half + 1) * BANK)
+            nc.vector.quantize_mx(out=mag_codes[0][:, cols].bitcast(FP8X4), scales=mag_plane[0][:, cols], in_=borrowed[half])
+        pick(LAST - 2, 0, M)
+        pick(LAST - 1, 0, M)
+        put(LAST)
+
         for m0 in range(0, M, CHUNK):
-            pick(ROW_TILES - 1, m0, CHUNK)
-            add_paste(1, offsets[1], m0)
-            magnitude(m0)
+            pick(LAST, m0, CHUNK)
+            add_paste(paste_tiles[1], m0)
+            magnitude(chunk(mag, m0), m0)
             if m0 > 0:
                 quantise(mag, mag_codes[1], mag_plane[1], m0 - CHUNK, m0)
             quantise(z, z_codes[1], z_plane[1], m0, m0 + CHUNK)

import math
from contextlib import ExitStack

import concourse.mybir as mybir
from concourse.masks import make_identity

K, H, N, T, S, M, T2 = 512, 1024, 768, 4096, 1024, 1024, 2048
FLOPS = 2 * (2 * K * H * S + 2 * H * N * M)

F32 = mybir.dt.float32
BF16 = mybir.dt.bfloat16
I32 = mybir.dt.int32
U32 = mybir.dt.uint32
U16 = mybir.dt.uint16
U8 = mybir.dt.uint8
FP8X4 = mybir.dt.float8_e4m3fn_x4
FP4X4 = mybir.dt.float4_e2m1fn_x4
ALU = mybir.AluOpType
ACT = mybir.ActivationFunctionType

P = 128
PACK = 4
PASS = P * PACK
PASSES = H // PASS
ROW_TILES = H // P
LAST = ROW_TILES - 1
BANK = 512
CHUNK = 256
LIST = 16
LINE = 4
QUANT_MAX = 1024


def tile_list_rework_pad_scores_kernel(
    tc, tab_words, tab_scales, offs, offs2, offs3, w1, w2_words, w2_scales, wgs, wgt, paste, w3_words, w3_scales, w4, out
):
    nc = tc.nc
    with ExitStack() as ctx:
        lists = ctx.enter_context(tc.tile_pool(name="lists", bufs=1))
        keep = ctx.enter_context(tc.tile_pool(name="keep", bufs=1))
        ring = ctx.enter_context(tc.tile_pool(name="ring", bufs=2))
        psum = ctx.enter_context(tc.psum_pool(name="psum", bufs=8))

        idx = lists.tile([P, S // LIST], U16, name="idx")
        idx2 = lists.tile([P, S // LIST], U16, name="idx2")
        idx3 = lists.tile([P, M // LIST], U16, name="idx3")

        def load_scale_rows(plane, rows):
            for quadrant in range(4):
                nc.sync.dma_start(
                    out=plane[32 * quadrant : 32 * quadrant + 4].bitcast(I32),
                    in_=rows[:, 4 * quadrant : 4 * quadrant + 4, :].rearrange("a r c -> r a c").bitcast(I32),
                )

        tab_plane = keep.tile([P, T], U8, name="tab_plane", align_bytes=64)
        w2_plane_raw = keep.tile([P, 1, H], U8, name="w2_plane_raw", align_bytes=64)
        w3_plane = keep.tile([P, PASSES, N], U8, name="w3_plane", align_bytes=64)
        nc.gpsimd.memset(tab_plane[:].bitcast(I32), 0)
        nc.gpsimd.memset(w2_plane_raw[:].bitcast(I32), 0)
        pages = [keep.tile([P, T2], F32, name="page%d" % n) for n in range(2)]
        for page in pages:
            nc.vector.memset(page[:], 0.0)
        nc.gpsimd.memset(w3_plane[:].bitcast(I32), 0)
        identity = keep.tile([P, P], F32, name="identity")
        make_identity(nc, identity[:])
        half_ln3 = keep.tile([P, 1], F32, name="half_ln3")
        nc.vector.memset(half_ln3[:], 1.0)
        nc.vector.tensor_scalar(half_ln3[:], half_ln3[:], 0.5 * math.log(3.0), None, ALU.mult)

        nc.sync.dma_start(idx[:], offs)
        w2_raw = keep.tile([P, 2 * H], U8, name="w2_raw")
        nc.sync.dma_start(out=w2_raw[:].bitcast(I32), in_=w2_words[0].bitcast(I32))
        load_scale_rows(tab_plane[:].rearrange("p (a t) -> p a t", a=1), tab_scales)
        tab = ring.tile([P, T], I32, name="tab", tag="wide")
        nc.sync.dma_start(out=tab[:], in_=tab_words[0].rearrange("p t i -> p (t i)").bitcast(I32))
        load_scale_rows(w2_plane_raw[:], w2_scales)
        w1_rows = w1.rearrange("(p j) r -> p j r", j=PACK)
        w1_raw = []
        put_factor = keep.tile([P, S], F32, name="put_factor")
        pick_factor = keep.tile([P, M], F32, name="pick_factor")
        for b in range(PASSES):
            raw = ring.tile([P, PACK, PASS], F32, name="w1_raw", tag="raw")
            nc.sync.dma_start(out=raw[:], in_=w1_rows[:, :, b * PASS : (b + 1) * PASS])
            w1_raw.append(raw)
            if b == 0:
                nc.sync.dma_start(idx2[:], offs2)
                nc.sync.dma_start(out=put_factor[:], in_=wgs)
        nc.sync.dma_start(idx3[:], offs3)
        nc.sync.dma_start(out=pick_factor[:], in_=wgt)

        w2_codes = keep.tile([P, 2 * H], U8, name="w2_codes", align_bytes=64)
        w2_plane = keep.tile([P, H], U8, name="w2_plane", align_bytes=64)
        nc.vector.tensor_copy(
            out=w2_codes[:].bitcast(U16).rearrange("p (b t q) -> p b t q", b=PASSES, t=PACK),
            in_=w2_raw[:].bitcast(U16).rearrange("p (b q t) -> p b t q", b=PASSES, t=PACK),
        )
        nc.vector.tensor_copy(
            out=w2_plane[:].rearrange("p (b t q) -> p b t q", b=PASSES, t=PACK),
            in_=w2_plane_raw[:, 0, :].rearrange("p (b q t) -> p b t q", b=PASSES, t=PACK),
        )

        v_codes = keep.tile([P, S], U32, name="v_codes", align_bytes=64)
        v_plane = keep.tile([P, S], U8, name="v_plane", align_bytes=64)
        nc.vector.tensor_copy(out=v_plane[:], in_=tab_plane[:].indirect(idx[:]))
        for s0 in range(0, S, BANK):
            entries = idx[:, s0 // LIST : (s0 + BANK) // LIST]
            nc.vector.tensor_copy(out=v_codes[:, s0 : s0 + BANK], in_=tab[:].bitcast(U32).indirect(entries))

        w1_codes = keep.tile([P, H], U32, name="w1_codes", align_bytes=64)
        w1_plane = keep.tile([P, H], U8, name="w1_plane", align_bytes=64)

        curves = [keep.tile([P, S], F32, name="curve%d" % n, align_bytes=64) for n in range(2)]
        feats = [keep.tile([P, S], F32, name="feat%d" % n, align_bytes=64) for n in range(2)]
        picked = [keep.tile([P, PACK, M], F32, name="picked%d" % b, align_bytes=64) for b in range(PASSES)]

        def quantise_w1(b, t0, t1, rounded, copy):
            copy(
                out=rounded.rearrange("p (t q j) -> p q j t", q=P, j=PACK),
                in_=w1_raw[b][:].rearrange("p j (q t) -> p q j t", t=PACK)[:, :, :, t0:t1],
            )
            cols = slice(b * PASS + t0 * P, b * PASS + t1 * P)
            nc.vector.quantize_mx(out=w1_codes[:, cols].bitcast(FP8X4), scales=w1_plane[:, cols], in_=rounded)

        first = ring.tile([P, P * PACK], BF16, name="w1_first", bufs=1, align_bytes=64)
        quantise_w1(0, 0, 1, first[:], nc.vector.tensor_copy)
        rounded = ring.tile([P, (PACK - 1) * P * PACK], BF16, name="w1_rounded", bufs=1, align_bytes=64)
        quantise_w1(0, 1, PACK, rounded[:], nc.scalar.copy)
        nc.vector.tensor_scalar(put_factor[:], put_factor[:], -2.0 / 3.0, None, ALU.mult)

        def row(k):
            return picked[k // PACK][:, k % PACK, :]

        def features(k):
            cols = slice(k * P, (k + 1) * P)
            curve = curves[k % 2]
            feat = feats[k % 2]
            for s0 in range(0, S, BANK):
                span = slice(s0, s0 + BANK)
                gate = psum.tile([P, BANK], F32, name="gate", tag="bank")
                nc.tensor.matmul_mx(
                    out=gate[:], lhsT=w2_codes[:, 2 * k * P : 2 * (k + 1) * P].bitcast(FP4X4), lhsT_scale=w2_plane[:, cols],
                    rhs=v_codes[:, span].bitcast(FP8X4), rhs_scale=v_plane[:, span], start=True, stop=True,
                )
                nc.scalar.activation(curve[:, span], gate[:], ACT.Tanh, bias=half_ln3[:], scale=0.5)
            for s0 in range(0, S, BANK):
                span = slice(s0, s0 + BANK)
                lin = psum.tile([P, BANK], F32, name="lin", tag="bank")
                nc.tensor.matmul_mx(
                    out=lin[:], lhsT=w1_codes[:, cols].bitcast(FP8X4), lhsT_scale=w1_plane[:, cols],
                    rhs=v_codes[:, span].bitcast(FP8X4), rhs_scale=v_plane[:, span], start=True, stop=True,
                )
                nc.vector.scalar_tensor_tensor(feat[:, span], curve[:, span], -2.0, lin[:], ALU.add, ALU.mult)

        def put(k):
            feat = feats[k % 2]
            width = BANK if k == 0 else S
            for s0 in range(0, S, width):
                entries = idx2[:, s0 // LIST : (s0 + width) // LIST]
                nc.vector.tensor_tensor(
                    pages[k % 2][:].indirect(entries), feat[:, s0 : s0 + width], put_factor[:, s0 : s0 + width], ALU.mult
                )

        def pick(k, m0, width):
            entries = idx3[:, m0 // LIST : (m0 + width) // LIST]
            nc.vector.tensor_tensor(
                row(k)[:, m0 : m0 + width], pages[k % 2][:].indirect(entries), pick_factor[:, m0 : m0 + width], ALU.mult
            )

        z_codes = [keep.tile([P, M], U32, name="z_codes%d" % b, align_bytes=64) for b in range(PASSES)]
        z_plane = [keep.tile([P, M], U8, name="z_plane%d" % b, align_bytes=64) for b in range(PASSES)]
        mag_codes = [keep.tile([P, M], U32, name="mag_codes%d" % b, align_bytes=64) for b in range(PASSES)]
        mag_plane = [keep.tile([P, M], U8, name="mag_plane%d" % b, align_bytes=64) for b in range(PASSES)]

        z = keep.tile([P, M * PACK], BF16, name="z", align_bytes=64)
        mag = keep.tile([P, M * PACK], BF16, name="mag", align_bytes=64)

        def chunk(values, m0):
            return values[:, m0 * PACK : (m0 + CHUNK) * PACK]

        def add_paste_turned(paste_rows, m0):
            back = psum.tile([P, CHUNK // P, 2, P], F32, name="back", tag="bank")
            for g in range(CHUNK // P):
                cols = slice(m0 + g * P, m0 + (g + 1) * P)
                total = psum.tile([P, PACK, P], F32, name="total", tag="bank")
                for t in range(PACK):
                    nc.tensor.matmul(total[:, t, :], row(t)[:, cols], identity[:], start=True, stop=False, is_transpose=True)
                    nc.tensor.matmul(total[:, t, :], paste_rows[:, t, cols], identity[:], start=False, stop=True, is_transpose=True)
                pairs = ring.tile([P, PACK * P], BF16, name="pairs", bufs=4)
                nc.scalar.copy(
                    out=pairs[:].rearrange("m (u p e) -> m u p e", u=2, e=2), in_=total[:].rearrange("m (u e) p -> m u p e", e=2)
                )
                for u in range(2):
                    nc.tensor.transpose(back[:, g, u, :], pairs[:].bitcast(F32)[:, u * P : (u + 1) * P], identity[:])
            nc.scalar.copy(
                out=chunk(z, m0).bitcast(F32).rearrange("p (g m u) -> p g m u", g=CHUNK // P, u=2),
                in_=back[:].rearrange("p g u m -> p g m u"),
            )

        def add_paste(paste_rows, m0):
            nc.vector.tensor_tensor(
                chunk(z, m0).rearrange("p (c i t) -> p c t i", i=LINE, t=PACK),
                picked[1][:, :, m0 : m0 + CHUNK].rearrange("p t (c i) -> p c t i", i=LINE),
                paste_rows[:, :, m0 : m0 + CHUNK].rearrange("p t (c i) -> p c t i", i=LINE),
                ALU.add,
            )

        def magnitude(into, m0):
            nc.scalar.activation(into, chunk(z, m0), ACT.Abs)

        def quantise(values, codes, plane, c0, c1):
            nc.vector.quantize_mx(out=codes[:, c0:c1].bitcast(FP8X4), scales=plane[:, c0:c1], in_=values[:, c0 * PACK : c1 * PACK])

        def load_paste(b):
            paste_rows = ring.tile([P, PACK, M], F32, name="paste_rows", tag="wide")
            nc.sync.dma_start(out=paste_rows[:], in_=paste[b * PASS : (b + 1) * PASS, :].rearrange("(p t) m -> p t m", t=PACK))
            return paste_rows

        w4_codes = keep.tile([P, PASSES * N], U32, name="w4_codes", align_bytes=64)
        w4_plane = keep.tile([P, PASSES * N], U8, name="w4_plane", align_bytes=64)

        def load_w4(b):
            raw = ring.tile([P, PACK, N], F32, name="w4_raw", tag="raw")
            nc.sync.dma_start(out=raw[:], in_=w4[b * PASS : (b + 1) * PASS, :].rearrange("(p j) n -> p j n", j=PACK))
            return raw

        w4_rounded = keep.tile([P, PASSES * N * PACK], BF16, name="w4_rounded", align_bytes=64)

        def round_w4(b, raw):
            nc.scalar.copy(
                out=w4_rounded[:, b * N * PACK : (b + 1) * N * PACK].rearrange("p (c i j) -> p c j i", i=LINE, j=PACK),
                in_=raw[:].rearrange("p j (c i) -> p c j i", i=LINE),
            )

        w3_codes = keep.tile([P, PASSES, 2 * N], U8, name="w3_codes", align_bytes=64)

        def scores(m0):
            span = slice(m0, m0 + CHUNK)
            for n0 in range(0, N, 2 * P):
                signed = psum.tile([P, 2, CHUNK], F32, name="signed", tag="bank")
                sized = psum.tile([P, 2, CHUNK], F32, name="sized", tag="bank")
                for b in range(PASSES):
                    for u in range(2):
                        n = n0 + u * P
                        nc.tensor.matmul_mx(
                            out=signed[:, u, :], lhsT=w3_codes[:, b, 2 * n : 2 * (n + P)].bitcast(FP4X4), lhsT_scale=w3_plane[:, b, n : n + P],
                            rhs=z_codes[b][:, span].bitcast(FP8X4), rhs_scale=z_plane[b][:, span],
                            start=(b == 0 and u == 0), stop=(b == PASSES - 1 and u == 1),
                        )
                for b in range(PASSES):
                    for u in range(2):
                        cols = slice(b * N + n0 + u * P, b * N + n0 + (u + 1) * P)
                        nc.tensor.matmul_mx(
                            out=sized[:, u, :], lhsT=w4_codes[:, cols].bitcast(FP8X4), lhsT_scale=w4_plane[:, cols],
                            rhs=mag_codes[b][:, span].bitcast(FP8X4), rhs_scale=mag_plane[b][:, span],
                            start=(b == 0 and u == 0), stop=(b == PASSES - 1 and u == 1),
                        )
                bounded = ring.tile([P, 2, CHUNK], F32, name="bounded", bufs=3)
                nc.scalar.activation(bounded[:], signed[:], ACT.Tanh)
                score = ring.tile([P, 2, CHUNK], F32, name="score", bufs=4)
                nc.vector.tensor_tensor(score[:], bounded[:], sized[:], ALU.add)
                nc.sync.dma_start(out=out[n0 : n0 + 2 * P, span].rearrange("(u p) m -> p u m", u=2), in_=score[:])

        features(0)
        paste_tiles = [load_paste(0)]
        for k in range(LAST):
            features(k + 1)
            put(k)
            if k == 0:
                paste_tiles.append(load_paste(1))
                w4_raw = [load_w4(b) for b in range(PASSES)]
                nc.sync.dma_start(out=w3_codes[:].bitcast(I32), in_=w3_words.rearrange("a p c -> p a c").bitcast(I32))
                load_scale_rows(w3_plane[:], w3_scales)
            if k == 1:
                rounded = ring.tile([P, PASS * PACK], BF16, name="w1_rounded", bufs=1, align_bytes=64)
                quantise_w1(1, 0, PACK, rounded[:], nc.scalar.copy)
            if 1 <= k < LAST - 1:
                pick(k - 1, 0, M)
            if 2 <= k < 2 + PASSES:
                round_w4(k - 2, w4_raw[k - 2])
            if k == 1 + PASSES:
                quantise(w4_rounded, w4_codes, w4_plane, 0, QUANT_MAX)
                quantise(w4_rounded, w4_codes, w4_plane, QUANT_MAX, PASSES * N)

        borrowed = [row(k).bitcast(BF16) for k in (LAST, LAST - 2)]
        for m0 in range(0, M, CHUNK):
            add_paste_turned(paste_tiles[0], m0)
            magnitude(chunk(borrowed[m0 // BANK], m0 % BANK), m0)
        quantise(z, z_codes[0], z_plane[0], 0, M)
        for half in range(2):
            cols = slice(half * BANK, (half + 1) * BANK)
            nc.vector.quantize_mx(out=mag_codes[0][:, cols].bitcast(FP8X4), scales=mag_plane[0][:, cols], in_=borrowed[half])
        pick(LAST - 2, 0, M)
        pick(LAST - 1, 0, M)
        put(LAST)

        for m0 in range(0, M, CHUNK):
            pick(LAST, m0, CHUNK)
            add_paste(paste_tiles[1], m0)
            magnitude(chunk(mag, m0), m0)
            if m0 > 0:
                quantise(mag, mag_codes[1], mag_plane[1], m0 - CHUNK, m0)
            quantise(z, z_codes[1], z_plane[1], m0, m0 + CHUNK)
            if m0 >= 2 * CHUNK:
                scores(m0 - 2 * CHUNK)
        quantise(mag, mag_codes[1], mag_plane[1], M - CHUNK, M)
        scores(M - 2 * CHUNK)
        scores(M - CHUNK)
